import numpy as np
import ml_dtypes


def mxq(x, axis, fmt="e4m3"):
    dtype, down = {"e4m3": (ml_dtypes.float8_e4m3fn, 7), "e5m2": (ml_dtypes.float8_e5m2, 14)}[fmt]
    v = np.moveaxis(np.asarray(x, np.float32).astype(ml_dtypes.bfloat16).astype(np.float64), axis, -1)
    blocks = v.reshape(v.shape[:-1] + (-1, 32))
    amax = np.abs(blocks).max(-1, keepdims=True)
    byte = np.maximum(np.where(amax > 0, np.frexp(amax)[1] - 1 + 127, 0) - down, 1)
    scale = np.exp2(byte - 127.0)
    codes = (blocks / scale).astype(np.float32).astype(dtype).astype(np.float64)
    return np.moveaxis((codes * scale).reshape(v.shape), -1, axis)


WIDE = False


def mx_kscale(k):
    if not WIDE:
        return np.ones(k)
    levels = np.array([10, -10, 5, -5, 0])
    if k % 512:
        return np.exp2(np.random.permutation(np.resize(levels, k // 32))).repeat(32)
    a = np.empty((k // 512, 16))
    for p in range(k // 512):
        a[p, :8] = np.random.permutation(np.resize(levels, 8))
        for g in range(8):
            far = levels[np.abs(levels - a[p, g]) >= 10]
            a[p, g + 8] = far[np.random.randint(len(far))]
    return np.exp2(a.ravel()).repeat(32)


def f64(x):
    return np.asarray(x).astype(np.float64)


def striped(idx):
    return np.tile(np.asarray(idx).reshape(-1, 16).T, (8, 1)).astype(np.uint16)


def unstriped(offs):
    return offs[:16].T.reshape(-1).astype(np.int64)


E2M1 = np.array([0.0, 0.5, 1.0, 1.5, 2.0, 3.0, 4.0, 6.0, -0.0, -0.5, -1.0, -1.5, -2.0, -3.0, -4.0, -6.0])


def pack_weight(w, fmt):
    k, n = w.shape
    w = f64(np.asarray(w, np.float32).astype(ml_dtypes.bfloat16)).reshape(k // 32, 32, n)
    amax = np.abs(w).max(1)
    if fmt == "e4m3":
        byte = np.frexp(amax)[1] - 1 + 127 - 7
    else:
        mant, ex = np.frexp(amax / 6.0)
        byte = np.where(mant > 0.5, ex, ex - 1) + 127
    byte = np.clip(np.where(amax > 0, byte, 1), 1, 254)
    scaled = (w * np.exp2(127.0 - byte)[:, None, :]).reshape(k, n).astype(np.float32)
    by_word = np.ascontiguousarray(scaled.reshape(k // 512, 128, 4, n).transpose(0, 1, 3, 2))
    if fmt == "e4m3":
        words = by_word.astype(ml_dtypes.float8_e4m3fn).view(np.uint8)
    else:
        c = by_word.astype(ml_dtypes.float4_e2m1fn).view(np.uint8) & 0xF
        words = (c[..., 0::2] | (c[..., 1::2] << 4)).reshape(k // 512, 128, 2 * n)
    return np.ascontiguousarray(words), np.ascontiguousarray(byte.astype(np.uint8).reshape(k // 512, 16, n))


def unpack_weight(words, scales, fmt):
    g, _, n = scales.shape
    words = np.ascontiguousarray(words).reshape(g, 128, n, -1)
    if fmt == "e4m3":
        vals = words.view(ml_dtypes.float8_e4m3fn).astype(np.float64)
    else:
        nib = np.empty((g, 128, n, 4), np.uint8)
        nib[..., 0::2] = words & 0xF
        nib[..., 1::2] = words >> 4
        vals = E2M1[nib]
    vals = vals * np.repeat(np.exp2(scales.astype(np.float64) - 127.0), 8, axis=1)[..., None]
    return vals.transpose(0, 1, 3, 2).reshape(g * 512, n)


def sigmoid(v):
    return 1.0 / (1.0 + np.exp(-v))


K, R, F, T, J = 512, 128, 512, 2048, 512


def setup_inputs():
    n = np.random.standard_normal
    idx = np.random.permutation(T)[:J]
    idx2 = np.random.permutation(T)[:J]
    fk = mx_kscale(K)
    ff = mx_kscale(F)
    tabp = pack_weight(n((K, T)) / fk[:, None], "e4m3")
    tab2p = pack_weight(n((K, T)) / fk[:, None], "e4m3")
    return {
        "tab_words": tabp[0],
        "tab_scales": tabp[1],
        "w1": (n((K, R)) * 1 / np.sqrt(K) * fk[:, None]).astype(np.float32),
        "tab2_words": tab2p[0],
        "tab2_scales": tab2p[1],
        "w2": (n((K, R)) * 1 / np.sqrt(K) * fk[:, None]).astype(np.float32),
        "bias": (np.random.uniform(-0.5, 0.5, (R, 1))).astype(np.float32),
        "wo": (n((F, R)) * 1 / np.sqrt(F) * ff[:, None]).astype(np.float32),
        "dy": (n((F, J)) / ff[:, None]).astype(np.float32),
        "og": (np.random.uniform(0.3, 1.0, (R, 1))).astype(np.float32),
        "base": (0.3 * n((R, J))).astype(np.float32),
        "offs": striped(idx),
        "offs2": striped(idx2),
    }


def reference(tab_words, tab_scales, w1, tab2_words, tab2_scales, w2, bias, wo, dy, og, base, offs, offs2):
    idx = unstriped(offs)
    idx2 = unstriped(offs2)
    tabu = unpack_weight(tab_words, tab_scales, "e4m3")
    tab2u = unpack_weight(tab2_words, tab2_scales, "e4m3")
    w1q = mxq(f64(w1), 0, "e4m3")
    tabidxg = tabu[:, idx]
    a = w1q.T @ tabidxg
    w2q = mxq(f64(w2), 0, "e4m3")
    tab2idx2g = tab2u[:, idx2]
    b = w2q.T @ tab2idx2g
    h1 = np.tanh(a)
    gt = sigmoid(b + f64(bias))
    woq = mxq(f64(wo), 0, "e4m3")
    dyq = mxq(f64(dy), 0, "e4m3")
    c0 = woq.T @ dyq
    dgt = c0 * h1
    db = dgt * gt * (1.0 - gt)
    hdb = db * 2.0
    hgt = hdb * (1.0 - gt) * dgt - hdb * dgt * gt
    hb = hgt * gt * (1.0 - gt)
    y = hb * f64(og) + f64(base)
    return y

@@ -1,0 +1,156 @@
+import math
+from contextlib import ExitStack
+
+import concourse.mybir as mybir
+
+K, R, F, T, J = 512, 128, 512, 2048, 512
+FLOPS = 3 * 2 * K * R * J
+
+F32 = mybir.dt.float32
+BF16 = mybir.dt.bfloat16
+I32 = mybir.dt.int32
+U32 = mybir.dt.uint32
+U16 = mybir.dt.uint16
+U8 = mybir.dt.uint8
+FP8X4 = mybir.dt.float8_e4m3fn_x4
+ACT = mybir.ActivationFunctionType
+ALU = mybir.AluOpType
+P = 128
+PACK = 4
+TAGS = {"w1r":"warm","tw1":"warm2","wor":"w2r","dyr0":"s2","dyr1":"tw2","dyr2":"warm","base_t":"s1"}
+
+
+def tile_attend_gptwotables_kernel(tc, tab_words, tab_scales, w1, tab2_words, tab2_scales, w2, bias, wo, dy, og, base, offs, offs2, out):
+    nc = tc.nc
+    with ExitStack() as ctx:
+        keep = ctx.enter_context(tc.tile_pool(name="keep", bufs=1))
+        psum = ctx.enter_context(tc.psum_pool(name="psum", bufs=1))
+
+        def sb(name, shape, dtype):
+            return keep.tile(shape, dtype, name=name, tag=TAGS.get(name, name), align_bytes=64)
+
+        def load_words(name, words, q):
+            t = sb(name, [P, T], I32)
+            q.dma_start(out=t[:], in_=words[0].rearrange("p n t -> p (n t)").bitcast(I32))
+            return t
+
+        def zero_plane(name, eng):
+            t = sb(name, [P, T], U8)
+            eng.memset(t[:].bitcast(I32), 0)
+            return t
+
+        def load_scales(t, scales, q, k0):
+            rows = scales[0].bitcast(I32)
+            for r in range(4):
+                q.dma_start(out=t[:].bitcast(I32)[k0 + r : P : 32, :], in_=rows[r : 16 : 4, :])
+
+        def load_rows(name, src, c0, c1, q):
+            t = sb(name, [P, PACK, c1 - c0], F32)
+            q.dma_start(out=t[:], in_=src.rearrange("(p t) c -> p t c", t=PACK)[:, :, c0:c1])
+            return t
+
+        def load_plain(name, src, shape, dtype, q):
+            t = sb(name, shape, dtype)
+            q.dma_start(out=t[:], in_=src)
+            return t
+
+        def weave(dst, raw, c0, c1, eng):
+            o = dst[:, c0:c1, :].rearrange("p (c i) t -> p c t i", i=4)
+            s = raw[:, :, c0:c1].rearrange("p t (c i) -> p c t i", i=4)
+            if eng == "v":
+                nc.vector.tensor_copy(out=o, in_=s)
+            elif eng == "g":
+                nc.gpsimd.tensor_scalar(out=o, in0=s, scalar1=1.0, scalar2=0.0, op0=ALU.mult, op1=ALU.add)
+            else:
+                nc.scalar.copy(out=o, in_=s)
+
+        def quant(name, woven, n):
+            codes = sb(name + "_codes", [P, n], U32)
+            sc = sb(name + "_sc", [P, n], U8)
+            nc.vector.quantize_mx(out=codes[:].bitcast(FP8X4), scales=sc[:], in_=woven[:].rearrange("p c t -> p (c t)"))
+            return codes, sc
+
+        def gather(name, window, lst, c0, c1, dtype):
+            g = sb(name, [P, c1 - c0], dtype)
+            w = window[:].bitcast(U32) if dtype == U32 else window[:]
+            nc.vector.tensor_copy(out=g[:], in_=w.indirect(lst[:, c0 // 16 : c1 // 16]))
+            return g
+
+        def mm(name, n, lhs, lhs_sc, rhs, rhs_sc):
+            acc = psum.tile([P, n], F32, name=name)
+            nc.tensor.matmul_mx(out=acc[:], lhsT=lhs.bitcast(FP8X4), lhsT_scale=lhs_sc, rhs=rhs.bitcast(FP8X4), rhs_scale=rhs_sc, start=True, stop=True)
+            return acc
+
+
+        s2 = zero_plane("s2", nc.vector)
+        warm = sb("warm", [P, 1], F32)
+        warm2 = sb("warm2", [P, 1], F32)
+        nc.vector.memset(warm[:], 0.0)
+        s1 = zero_plane("s1", nc.vector)
+
+        l2 = load_plain("l2", offs2, [P, J // 16], U16, nc.sync)
+        l1 = load_plain("l1", offs, [P, J // 16], U16, nc.sync)
+        w2r = load_rows("w2r", w2, 0, R, nc.sync)
+        tw2 = load_words("tw2", tab2_words, nc.sync)
+        load_scales(s2, tab2_scales, nc.scalar, 0)
+        nc.scalar.activation(out=warm2[:], in_=warm[:], func=ACT.Tanh)
+        load_scales(s1, tab_scales, nc.scalar, 4)
+        bias_t = load_plain("bias_t", bias, [P, 1], F32, nc.gpsimd)
+        og_t = load_plain("og_t", og, [P, 1], F32, nc.gpsimd)
+        w1r = load_rows("w1r", w1, 0, R, nc.sync)
+        tw1 = load_words("tw1", tab_words, nc.sync)
+
+        nb = sb("nb", [P, 1], F32)
+        nc.gpsimd.tensor_scalar(out=nb[:], in0=bias_t[:], scalar1=-0.5, scalar2=0.0, op0=ALU.mult, op1=ALU.add)
+
+        w2w = sb("w2w", [P, R, PACK], BF16)
+        weave(w2w, w2r, 0, R, "s")
+        wor = load_rows("wor", wo, 0, R, nc.sync)
+        gs2 = gather("gs2", s2, l2, 0, J, U8)
+        cuts = [0, 256, 384, 512]
+        dyr = [load_rows("dyr0", dy, cuts[0], cuts[1], nc.sync)]
+        gw2 = gather("gw2", tw2, l2, 0, J, U32)
+        dyr.append(load_rows("dyr1", dy, cuts[1], cuts[2], nc.sync))
+        w2c, w2s = quant("w2q", w2w, R)
+        bacc = mm("bacc", J, w2c[:], w2s[:], gw2[:], gs2[:])
+        w1w = sb("w1w", [P, R, PACK], BF16)
+        weave(w1w, w1r, 0, R, "s")
+        dyr.append(load_rows("dyr2", dy, cuts[2], cuts[3], nc.sync))
+        gs1 = gather("gs1", s1, l1, 0, J, U8)
+        base_t = load_plain("base_t", base, [P, J], F32, nc.sync)
+        w1c, w1s = quant("w1q", w1w, R)
+        tn = sb("tn", [P, J], F32)
+        nc.scalar.activation(out=tn[:], in_=bacc[:], func=ACT.Tanh, bias=nb[:], scale=-0.5)
+        q = sb("q", [P, J], F32)
+        nc.scalar.activation(out=q[:], in_=tn[:], func=ACT.Square)
+        halves = [0, 256, 512]
+        gw1 = [gather("gw1_%d" % i, tw1, l1, halves[i], halves[i + 1], U32) for i in range(2)]
+        wow = sb("wow", [P, R, PACK], BF16)
+        weave(wow, wor, 0, R, "s")
+        woc, wos = quant("woq", wow, R)
+        h = sb("h", [P, J], F32)
+        m = sb("m", [P, J], F32)
+        for i in range(2):
+            hs = slice(halves[i], halves[i + 1])
+            acc = mm("aacc%d" % i, 256, w1c[:], w1s[:], gw1[i][:], gs1[4:P, hs])
+            nc.scalar.activation(out=h[:, hs], in_=acc[:], func=ACT.Tanh)
+            nc.vector.scalar_tensor_tensor(out=m[:, hs], in0=q[:, hs], scalar=-1.0, in1=h[:, hs], op0=ALU.add, op1=ALU.mult)
+        d = sb("d", [P, J], F32)
+        d2 = sb("d2", [P, J], F32)
+        r = sb("r", [P, J], F32)
+        res = sb("res", [P, J], F32)
+        share = [128, 128, 64]
+        for i in range(3):
+            n = cuts[i + 1] - cuts[i]
+            cs = slice(cuts[i], cuts[i + 1])
+            dw = sb("dw%d" % i, [P, n, PACK], BF16)
+            weave(dw, dyr[i], 0, share[i], "s")
+            if share[i] < n:
+                weave(dw, dyr[i], share[i], n, "v")
+            dc, ds = quant("dq%d" % i, dw, n)
+            acc = mm("cacc%d" % i, n, woc[:], wos[:], dc[:], ds[:])
+            nc.vector.tensor_tensor(out=d[:, cs], in0=acc[:], in1=m[:, cs], op=ALU.mult)
+            nc.scalar.activation(out=d2[:, cs], in_=d[:, cs], func=ACT.Square, scale=math.sqrt(0.125))
+            nc.vector.scalar_tensor_tensor(out=r[:, cs], in0=tn[:, cs], scalar=og_t[:], in1=d2[:, cs], op0=ALU.mult, op1=ALU.mult)
+            nc.vector.tensor_tensor(out=res[:, cs], in0=r[:, cs], in1=base_t[:, cs], op=ALU.add)
+            nc.sync.dma_start(out=out[:, cs], in_=res[:, cs])

@@ -17,7 +17,7 @@ ACT = mybir.ActivationFunctionType
 ALU = mybir.AluOpType
 P = 128
 PACK = 4
-TAGS = {"w1r":"warm","tw1":"warm2","wor":"w2r","dyr0":"s2","dyr1":"tw2","dyr2":"warm","base_t":"s1"}
+TAGS = {"pt":"tw1","qb":"dw2"}
 
 
 def tile_attend_gptwotables_kernel(tc, tab_words, tab_scales, w1, tab2_words, tab2_scales, w2, bias, wo, dy, og, base, offs, offs2, out):
@@ -82,75 +82,84 @@ def tile_attend_gptwotables_kernel(tc, tab_words, tab_scales, w1, tab2_words, ta
             return acc
 
 
-        s2 = zero_plane("s2", nc.vector)
+        s2 = zero_plane("s2", nc.gpsimd)
+        s1 = zero_plane("s1", nc.vector)
         warm = sb("warm", [P, 1], F32)
         warm2 = sb("warm2", [P, 1], F32)
         nc.vector.memset(warm[:], 0.0)
-        s1 = zero_plane("s1", nc.vector)
+        nc.scalar.activation(out=warm2[:], in_=warm[:], func=ACT.Tanh)
 
         l2 = load_plain("l2", offs2, [P, J // 16], U16, nc.sync)
-        l1 = load_plain("l1", offs, [P, J // 16], U16, nc.sync)
         w2r = load_rows("w2r", w2, 0, R, nc.sync)
+        w1r = load_rows("w1r", w1, 0, R, nc.sync)
+        load_scales(s2, tab2_scales, nc.sync, 0)
         tw2 = load_words("tw2", tab2_words, nc.sync)
-        load_scales(s2, tab2_scales, nc.scalar, 0)
-        nc.scalar.activation(out=warm2[:], in_=warm[:], func=ACT.Tanh)
-        load_scales(s1, tab_scales, nc.scalar, 4)
+        l1 = load_plain("l1", offs, [P, J // 16], U16, nc.sync)
+        load_scales(s1, tab_scales, nc.sync, 4)
+        tw1 = load_words("tw1", tab_words, nc.sync)
+        wor = load_rows("wor", wo, 0, R, nc.sync)
+        cuts = [0,256,384,512]
+        dyr = [load_rows("dyr%d" % i, dy, cuts[i], cuts[i + 1], nc.sync) for i in range(len(cuts) - 1)]
+        base_t = load_plain("base_t", base, [P, J], F32, nc.sync)
         bias_t = load_plain("bias_t", bias, [P, 1], F32, nc.gpsimd)
         og_t = load_plain("og_t", og, [P, 1], F32, nc.gpsimd)
-        w1r = load_rows("w1r", w1, 0, R, nc.sync)
-        tw1 = load_words("tw1", tab_words, nc.sync)
 
         nb = sb("nb", [P, 1], F32)
         nc.gpsimd.tensor_scalar(out=nb[:], in0=bias_t[:], scalar1=-0.5, scalar2=0.0, op0=ALU.mult, op1=ALU.add)
-
+        halves = [slice(0, 256), slice(256, 512)]
         w2w = sb("w2w", [P, R, PACK], BF16)
         weave(w2w, w2r, 0, R, "s")
-        wor = load_rows("wor", wo, 0, R, nc.sync)
-        gs2 = gather("gs2", s2, l2, 0, J, U8)
-        cuts = [0, 256, 384, 512]
-        dyr = [load_rows("dyr0", dy, cuts[0], cuts[1], nc.sync)]
-        gw2 = gather("gw2", tw2, l2, 0, J, U32)
-        dyr.append(load_rows("dyr1", dy, cuts[1], cuts[2], nc.sync))
-        w2c, w2s = quant("w2q", w2w, R)
-        bacc = mm("bacc", J, w2c[:], w2s[:], gw2[:], gs2[:])
         w1w = sb("w1w", [P, R, PACK], BF16)
         weave(w1w, w1r, 0, R, "s")
-        dyr.append(load_rows("dyr2", dy, cuts[2], cuts[3], nc.sync))
-        gs1 = gather("gs1", s1, l1, 0, J, U8)
-        base_t = load_plain("base_t", base, [P, J], F32, nc.sync)
+        gs2 = gather("gs2", s2, l2, 0, J, U8)
+        w2c, w2s = quant("w2q", w2w, R)
         w1c, w1s = quant("w1q", w1w, R)
         tn = sb("tn", [P, J], F32)
-        nc.scalar.activation(out=tn[:], in_=bacc[:], func=ACT.Tanh, bias=nb[:], scale=-0.5)
+        for i, hs in enumerate(halves):
+            g = gather("gw2_%d" % i, tw2, l2, hs.start, hs.stop, U32)
+            acc = mm("bacc%d" % i, 256, w2c[:], w2s[:], g[:], gs2[:, hs])
+            nc.scalar.activation(out=tn[:, hs], in_=acc[:], func=ACT.Tanh, bias=nb[:], scale=-0.5)
+        gs1 = gather("gs1", s1, l1, 0, J, U8)
         q = sb("q", [P, J], F32)
         nc.scalar.activation(out=q[:], in_=tn[:], func=ACT.Square)
-        halves = [0, 256, 512]
-        gw1 = [gather("gw1_%d" % i, tw1, l1, halves[i], halves[i + 1], U32) for i in range(2)]
+        u = sb("u", [P, J], F32)
+        root = math.sqrt(0.125)
+        nc.scalar.activation(out=u[:], in_=q[:], func=ACT.Square, bias=root, scale=-root)
+        gw1 = [gather("gw1_%d" % i, tw1, l1, hs.start, hs.stop, U32) for i, hs in enumerate(halves)]
         wow = sb("wow", [P, R, PACK], BF16)
         weave(wow, wor, 0, R, "s")
         woc, wos = quant("woq", wow, R)
+        pt = sb("pt", [P, J], F32)
+        nc.vector.tensor_tensor(out=pt[:], in0=tn[:], in1=u[:], op=ALU.mult)
         h = sb("h", [P, J], F32)
-        m = sb("m", [P, J], F32)
-        for i in range(2):
-            hs = slice(halves[i], halves[i + 1])
+        h2 = sb("h2", [P, J], F32)
+        for i, hs in enumerate(halves):
             acc = mm("aacc%d" % i, 256, w1c[:], w1s[:], gw1[i][:], gs1[4:P, hs])
             nc.scalar.activation(out=h[:, hs], in_=acc[:], func=ACT.Tanh)
-            nc.vector.scalar_tensor_tensor(out=m[:, hs], in0=q[:, hs], scalar=-1.0, in1=h[:, hs], op0=ALU.add, op1=ALU.mult)
-        d = sb("d", [P, J], F32)
-        d2 = sb("d2", [P, J], F32)
+        for hs in halves:
+            nc.scalar.activation(out=h2[:, hs], in_=h[:, hs], func=ACT.Square)
+        qa = sb("qa", [P, 256], F32)
+        nc.vector.tensor_tensor(out=qa[:], in0=h2[:, halves[0]], in1=pt[:, halves[0]], op=ALU.mult)
+        c2 = sb("c2", [P, J], F32)
         r = sb("r", [P, J], F32)
         res = sb("res", [P, J], F32)
-        share = [128, 128, 64]
-        for i in range(3):
+        share = [64,128,64]
+        accs = []
+        for i in range(len(cuts) - 1):
             n = cuts[i + 1] - cuts[i]
-            cs = slice(cuts[i], cuts[i + 1])
             dw = sb("dw%d" % i, [P, n, PACK], BF16)
-            weave(dw, dyr[i], 0, share[i], "s")
+            if share[i] > 0:
+                weave(dw, dyr[i], 0, share[i], "s")
             if share[i] < n:
                 weave(dw, dyr[i], share[i], n, "v")
             dc, ds = quant("dq%d" % i, dw, n)
-            acc = mm("cacc%d" % i, n, woc[:], wos[:], dc[:], ds[:])
-            nc.vector.tensor_tensor(out=d[:, cs], in0=acc[:], in1=m[:, cs], op=ALU.mult)
-            nc.scalar.activation(out=d2[:, cs], in_=d[:, cs], func=ACT.Square, scale=math.sqrt(0.125))
-            nc.vector.scalar_tensor_tensor(out=r[:, cs], in0=tn[:, cs], scalar=og_t[:], in1=d2[:, cs], op0=ALU.mult, op1=ALU.mult)
-            nc.vector.tensor_tensor(out=res[:, cs], in0=r[:, cs], in1=base_t[:, cs], op=ALU.add)
+            accs.append(mm("cacc%d" % i, n, woc[:], wos[:], dc[:], ds[:]))
+        qb = sb("qb", [P, 256], F32)
+        nc.vector.tensor_tensor(out=qb[:], in0=h2[:, halves[1]], in1=pt[:, halves[1]], op=ALU.mult)
+        qs = [qa[:] if c < 256 else qb[:, c - 256 : e - 256] for c, e in zip(cuts, cuts[1:])]
+        pieces = [slice(cuts[i], cuts[i + 1]) for i in range(len(cuts) - 1)]
+        for i, cs in enumerate(pieces):
+            nc.scalar.activation(out=c2[:, cs], in_=accs[i][:], func=ACT.Square)
+            nc.vector.tensor_tensor(out=r[:, cs], in0=c2[:, cs], in1=qs[i], op=ALU.mult)
+            nc.vector.scalar_tensor_tensor(out=res[:, cs], in0=r[:, cs], scalar=og_t[:], in1=base_t[:, cs], op0=ALU.mult, op1=ALU.add)
             nc.sync.dma_start(out=out[:, cs], in_=res[:, cs])

@@ -17,7 +17,7 @@ ACT = mybir.ActivationFunctionType
 ALU = mybir.AluOpType
 P = 128
 PACK = 4
-TAGS = {"pt":"tw1","qb":"dw2"}
+TAGS = {"qq":"tw1","dq_codes":"s1"}
 
 
 def tile_attend_gptwotables_kernel(tc, tab_words, tab_scales, w1, tab2_words, tab2_scales, w2, bias, wo, dy, og, base, offs, offs2, out):
@@ -90,76 +90,74 @@ def tile_attend_gptwotables_kernel(tc, tab_words, tab_scales, w1, tab2_words, ta
         nc.scalar.activation(out=warm2[:], in_=warm[:], func=ACT.Tanh)
 
         l2 = load_plain("l2", offs2, [P, J // 16], U16, nc.sync)
-        w2r = load_rows("w2r", w2, 0, R, nc.sync)
-        w1r = load_rows("w1r", w1, 0, R, nc.sync)
-        load_scales(s2, tab2_scales, nc.sync, 0)
-        tw2 = load_words("tw2", tab2_words, nc.sync)
-        l1 = load_plain("l1", offs, [P, J // 16], U16, nc.sync)
-        load_scales(s1, tab_scales, nc.sync, 4)
-        tw1 = load_words("tw1", tab_words, nc.sync)
         wor = load_rows("wor", wo, 0, R, nc.sync)
-        cuts = [0,256,384,512]
-        dyr = [load_rows("dyr%d" % i, dy, cuts[i], cuts[i + 1], nc.sync) for i in range(len(cuts) - 1)]
+        w2r = load_rows("w2r", w2, 0, R, nc.sync)
+        load_scales(s2, tab2_scales, nc.sync, 0)
+        dyr = load_rows("dyr", dy, 0, J, nc.sync)
+        l1 = load_plain("l1", offs, [P, J // 16], U16, nc.sync)
+        tw2 = load_words("tw2", tab2_words, nc.sync)
+        w1r = load_rows("w1r", w1, 0, R, nc.sync)
+        tw1 = load_words("tw1", tab_words, nc.sync)
         base_t = load_plain("base_t", base, [P, J], F32, nc.sync)
+        load_scales(s1, tab_scales, nc.gpsimd, 4)
         bias_t = load_plain("bias_t", bias, [P, 1], F32, nc.gpsimd)
         og_t = load_plain("og_t", og, [P, 1], F32, nc.gpsimd)
 
         nb = sb("nb", [P, 1], F32)
         nc.gpsimd.tensor_scalar(out=nb[:], in0=bias_t[:], scalar1=-0.5, scalar2=0.0, op0=ALU.mult, op1=ALU.add)
         halves = [slice(0, 256), slice(256, 512)]
-        w2w = sb("w2w", [P, R, PACK], BF16)
-        weave(w2w, w2r, 0, R, "s")
-        w1w = sb("w1w", [P, R, PACK], BF16)
-        weave(w1w, w1r, 0, R, "s")
-        gs2 = gather("gs2", s2, l2, 0, J, U8)
-        w2c, w2s = quant("w2q", w2w, R)
-        w1c, w1s = quant("w1q", w1w, R)
-        tn = sb("tn", [P, J], F32)
-        for i, hs in enumerate(halves):
-            g = gather("gw2_%d" % i, tw2, l2, hs.start, hs.stop, U32)
-            acc = mm("bacc%d" % i, 256, w2c[:], w2s[:], g[:], gs2[:, hs])
-            nc.scalar.activation(out=tn[:, hs], in_=acc[:], func=ACT.Tanh, bias=nb[:], scale=-0.5)
-        gs1 = gather("gs1", s1, l1, 0, J, U8)
-        q = sb("q", [P, J], F32)
-        nc.scalar.activation(out=q[:], in_=tn[:], func=ACT.Square)
-        u = sb("u", [P, J], F32)
-        root = math.sqrt(0.125)
-        nc.scalar.activation(out=u[:], in_=q[:], func=ACT.Square, bias=root, scale=-root)
-        gw1 = [gather("gw1_%d" % i, tw1, l1, hs.start, hs.stop, U32) for i, hs in enumerate(halves)]
         wow = sb("wow", [P, R, PACK], BF16)
         weave(wow, wor, 0, R, "s")
+        w2w = sb("w2w", [P, R, PACK], BF16)
+        weave(w2w, w2r, 0, R, "s")
+        gs2 = gather("gs2", s2, l2, 0, J, U8)
         woc, wos = quant("woq", wow, R)
+        w2c, w2s = quant("w2q", w2w, R)
+        dw = sb("dw", [P, J, PACK], BF16)
+        weave(dw, dyr, 0, 320, "s")
+        weave(dw, dyr, 320, J, "v")
+        gs1 = gather("gs1", s1, l1, 0, J, U8)
+        dc, ds = quant("dq", dw, J)
+        cacc = mm("cacc", J, woc[:], wos[:], dc[:], ds[:])
+        c2 = sb("c2", [P, J], F32)
+        nc.scalar.activation(out=c2[:], in_=cacc[:], func=ACT.Square)
+        tn = sb("tn", [P, J], F32)
+        baccs = []
+        for i, hs in enumerate(halves):
+            g = gather("gw2_%d" % i, tw2, l2, hs.start, hs.stop, U32)
+            baccs.append(mm("bacc%d" % i, 256, w2c[:], w2s[:], g[:], gs2[:, hs]))
+        w1w = sb("w1w", [P, R, PACK], BF16)
+        weave(w1w, w1r, 0, R, "v")
+        w1c, w1s = quant("w1q", w1w, R)
+        q = sb("q", [P, J], F32)
+        u = sb("u", [P, J], F32)
+        root = math.sqrt(0.125)
+        for i, hs in enumerate(halves):
+            nc.scalar.activation(out=tn[:, hs], in_=baccs[i][:], func=ACT.Tanh, bias=nb[:], scale=-0.5)
+        for hs in halves:
+            nc.scalar.activation(out=q[:, hs], in_=tn[:, hs], func=ACT.Square)
+        for hs in halves:
+            nc.scalar.activation(out=u[:, hs], in_=q[:, hs], func=ACT.Square, bias=root, scale=-root)
+        gw1 = [gather("gw1_%d" % i, tw1, l1, hs.start, hs.stop, U32) for i, hs in enumerate(halves)]
         pt = sb("pt", [P, J], F32)
-        nc.vector.tensor_tensor(out=pt[:], in0=tn[:], in1=u[:], op=ALU.mult)
+        qq = sb("qq", [P, J], F32)
+        for hs in halves:
+            nc.vector.tensor_tensor(out=pt[:, hs], in0=tn[:, hs], in1=c2[:, hs], op=ALU.mult)
+        for hs in halves:
+            nc.vector.tensor_tensor(out=qq[:, hs], in0=pt[:, hs], in1=u[:, hs], op=ALU.mult)
         h = sb("h", [P, J], F32)
         h2 = sb("h2", [P, J], F32)
-        for i, hs in enumerate(halves):
-            acc = mm("aacc%d" % i, 256, w1c[:], w1s[:], gw1[i][:], gs1[4:P, hs])
-            nc.scalar.activation(out=h[:, hs], in_=acc[:], func=ACT.Tanh)
-        for hs in halves:
-            nc.scalar.activation(out=h2[:, hs], in_=h[:, hs], func=ACT.Square)
-        qa = sb("qa", [P, 256], F32)
-        nc.vector.tensor_tensor(out=qa[:], in0=h2[:, halves[0]], in1=pt[:, halves[0]], op=ALU.mult)
-        c2 = sb("c2", [P, J], F32)
         r = sb("r", [P, J], F32)
         res = sb("res", [P, J], F32)
-        share = [64,128,64]
-        accs = []
-        for i in range(len(cuts) - 1):
-            n = cuts[i + 1] - cuts[i]
-            dw = sb("dw%d" % i, [P, n, PACK], BF16)
-            if share[i] > 0:
-                weave(dw, dyr[i], 0, share[i], "s")
-            if share[i] < n:
-                weave(dw, dyr[i], share[i], n, "v")
-            dc, ds = quant("dq%d" % i, dw, n)
-            accs.append(mm("cacc%d" % i, n, woc[:], wos[:], dc[:], ds[:]))
-        qb = sb("qb", [P, 256], F32)
-        nc.vector.tensor_tensor(out=qb[:], in0=h2[:, halves[1]], in1=pt[:, halves[1]], op=ALU.mult)
-        qs = [qa[:] if c < 256 else qb[:, c - 256 : e - 256] for c, e in zip(cuts, cuts[1:])]
-        pieces = [slice(cuts[i], cuts[i + 1]) for i in range(len(cuts) - 1)]
+        cuts = [0,256,384,512]
+        pieces = [slice(c, e) for c, e in zip(cuts, cuts[1:])]
         for i, cs in enumerate(pieces):
-            nc.scalar.activation(out=c2[:, cs], in_=accs[i][:], func=ACT.Square)
-            nc.vector.tensor_tensor(out=r[:, cs], in0=c2[:, cs], in1=qs[i], op=ALU.mult)
+            g = gw1[cs.start // 256][:, cs.start % 256 : cs.start % 256 + cs.stop - cs.start]
+            acc = mm("aacc%d" % i, cs.stop - cs.start, w1c[:], w1s[:], g, gs1[4:P, cs])
+            nc.scalar.activation(out=h[:, cs], in_=acc[:], func=ACT.Tanh)
+            nc.scalar.activation(out=h2[:, cs], in_=h[:, cs], func=ACT.Square)
+
+        for cs in pieces:
+            nc.vector.tensor_tensor(out=r[:, cs], in0=h2[:, cs], in1=qq[:, cs], op=ALU.mult)
             nc.vector.scalar_tensor_tensor(out=res[:, cs], in0=r[:, cs], scalar=og_t[:], in1=base_t[:, cs], op0=ALU.mult, op1=ALU.add)
             nc.sync.dma_start(out=out[:, cs], in_=res[:, cs])

@@ -17,7 +17,7 @@ ACT = mybir.ActivationFunctionType
 ALU = mybir.AluOpType
 P = 128
 PACK = 4
-TAGS = {"qq":"tw1","dq_codes":"s1"}
+TAGS = {"qq":"tw1","tn":"w1r"}
 
 
 def tile_attend_gptwotables_kernel(tc, tab_words, tab_scales, w1, tab2_words, tab2_scales, w2, bias, wo, dy, og, base, offs, offs2, out):
@@ -96,10 +96,10 @@ def tile_attend_gptwotables_kernel(tc, tab_words, tab_scales, w1, tab2_words, ta
         dyr = load_rows("dyr", dy, 0, J, nc.sync)
         l1 = load_plain("l1", offs, [P, J // 16], U16, nc.sync)
         tw2 = load_words("tw2", tab2_words, nc.sync)
+        load_scales(s1, tab_scales, nc.sync, 4)
         w1r = load_rows("w1r", w1, 0, R, nc.sync)
         tw1 = load_words("tw1", tab_words, nc.sync)
         base_t = load_plain("base_t", base, [P, J], F32, nc.sync)
-        load_scales(s1, tab_scales, nc.gpsimd, 4)
         bias_t = load_plain("bias_t", bias, [P, 1], F32, nc.gpsimd)
         og_t = load_plain("og_t", og, [P, 1], F32, nc.gpsimd)
 
@@ -114,9 +114,8 @@ def tile_attend_gptwotables_kernel(tc, tab_words, tab_scales, w1, tab2_words, ta
         woc, wos = quant("woq", wow, R)
         w2c, w2s = quant("w2q", w2w, R)
         dw = sb("dw", [P, J, PACK], BF16)
-        weave(dw, dyr, 0, 320, "s")
-        weave(dw, dyr, 320, J, "v")
-        gs1 = gather("gs1", s1, l1, 0, J, U8)
+        weave(dw, dyr, 0, 192, "s")
+        weave(dw, dyr, 192, J, "v")
         dc, ds = quant("dq", dw, J)
         cacc = mm("cacc", J, woc[:], wos[:], dc[:], ds[:])
         c2 = sb("c2", [P, J], F32)
@@ -127,7 +126,8 @@ def tile_attend_gptwotables_kernel(tc, tab_words, tab_scales, w1, tab2_words, ta
             g = gather("gw2_%d" % i, tw2, l2, hs.start, hs.stop, U32)
             baccs.append(mm("bacc%d" % i, 256, w2c[:], w2s[:], g[:], gs2[:, hs]))
         w1w = sb("w1w", [P, R, PACK], BF16)
-        weave(w1w, w1r, 0, R, "v")
+        weave(w1w, w1r, 0, R, "s")
+        gs1 = gather("gs1", s1, l1, 0, J, U8)
         w1c, w1s = quant("w1q", w1w, R)
         q = sb("q", [P, J], F32)
         u = sb("u", [P, J], F32)
@@ -149,15 +149,17 @@ def tile_attend_gptwotables_kernel(tc, tab_words, tab_scales, w1, tab2_words, ta
         h2 = sb("h2", [P, J], F32)
         r = sb("r", [P, J], F32)
         res = sb("res", [P, J], F32)
-        cuts = [0,256,384,512]
+        cuts = [0,128,256,384,512]
         pieces = [slice(c, e) for c, e in zip(cuts, cuts[1:])]
-        for i, cs in enumerate(pieces):
-            g = gw1[cs.start // 256][:, cs.start % 256 : cs.start % 256 + cs.stop - cs.start]
-            acc = mm("aacc%d" % i, cs.stop - cs.start, w1c[:], w1s[:], g, gs1[4:P, cs])
-            nc.scalar.activation(out=h[:, cs], in_=acc[:], func=ACT.Tanh)
-            nc.scalar.activation(out=h2[:, cs], in_=h[:, cs], func=ACT.Square)
-
-        for cs in pieces:
-            nc.vector.tensor_tensor(out=r[:, cs], in0=h2[:, cs], in1=qq[:, cs], op=ALU.mult)
-            nc.vector.scalar_tensor_tensor(out=res[:, cs], in0=r[:, cs], scalar=og_t[:], in1=base_t[:, cs], op0=ALU.mult, op1=ALU.add)
-            nc.sync.dma_start(out=out[:, cs], in_=res[:, cs])
+        for half in range(2):
+            pair = pieces[2 * half : 2 * half + 2]
+            for i, cs in enumerate(pair):
+                acc = mm("aacc%d" % (2 * half + i), 128, w1c[:], w1s[:], gw1[half][:, 128 * i : 128 * (i + 1)], gs1[4:P, cs])
+                nc.scalar.activation(out=h[:, cs], in_=acc[:], func=ACT.Tanh)
+            for cs in pair:
+                nc.scalar.activation(out=h2[:, cs], in_=h[:, cs], func=ACT.Square)
+            for cs in pair:
+                nc.vector.tensor_tensor(out=r[:, cs], in0=h2[:, cs], in1=qq[:, cs], op=ALU.mult)
+            for cs in pair:
+                nc.vector.scalar_tensor_tensor(out=res[:, cs], in0=r[:, cs], scalar=og_t[:], in1=base_t[:, cs], op0=ALU.mult, op1=ALU.add)
+            nc.sync.dma_start(out=out[:, halves[half]], in_=res[:, halves[half]])

@@ -3,7 +3,7 @@ from contextlib import ExitStack
 
 import concourse.mybir as mybir
 
-K, R, F, T, J = 512, 128, 512, 2048, 512
+K, R, T, J = 512, 128, 2048, 512
 FLOPS = 3 * 2 * K * R * J
 
 F32 = mybir.dt.float32
@@ -15,9 +15,18 @@ U8 = mybir.dt.uint8
 FP8X4 = mybir.dt.float8_e4m3fn_x4
 ACT = mybir.ActivationFunctionType
 ALU = mybir.AluOpType
+
 P = 128
+QUADRANT = 32
+BLOCKS = K // 32
 PACK = 4
-TAGS = {"qq":"tw1","tn":"w1r"}
+LINE = 4
+PER_COLUMN = 16
+TAB_FIRST = 4
+
+HALVES = [slice(0, J // 2), slice(J // 2, J)]
+CHUNKS = [slice(0, 256), slice(256, 384), slice(384, 512)]
+ON_SCALAR = [128, 128, 64]
 
 
 def tile_attend_gptwotables_kernel(tc, tab_words, tab_scales, w1, tab2_words, tab2_scales, w2, bias, wo, dy, og, base, offs, offs2, out):
@@ -26,140 +35,130 @@ def tile_attend_gptwotables_kernel(tc, tab_words, tab_scales, w1, tab2_words, ta
         keep = ctx.enter_context(tc.tile_pool(name="keep", bufs=1))
         psum = ctx.enter_context(tc.psum_pool(name="psum", bufs=1))
 
-        def sb(name, shape, dtype):
-            return keep.tile(shape, dtype, name=name, tag=TAGS.get(name, name), align_bytes=64)
+        def sbuf(name, shape, dtype):
+            return keep.tile(shape, dtype, name=name, align_bytes=64)
 
-        def load_words(name, words, q):
-            t = sb(name, [P, T], I32)
-            q.dma_start(out=t[:], in_=words[0].rearrange("p n t -> p (n t)").bitcast(I32))
-            return t
+        def load(name, src, shape, dtype, queue):
+            tile = sbuf(name, shape, dtype)
+            queue.dma_start(out=tile[:], in_=src)
+            return tile
 
-        def zero_plane(name, eng):
-            t = sb(name, [P, T], U8)
-            eng.memset(t[:].bitcast(I32), 0)
-            return t
+        def load_words(name, words):
+            return load(name, words[0].rearrange("p n t -> p (n t)").bitcast(I32), [P, T], I32, nc.sync)
 
-        def load_scales(t, scales, q, k0):
+        def zeroed_plane(name, engine):
+            plane = sbuf(name, [P, T], U8)
+            engine.memset(plane[:].bitcast(I32), 0)
+            return plane
+
+        def load_scale_rows(plane, scales, first):
             rows = scales[0].bitcast(I32)
-            for r in range(4):
-                q.dma_start(out=t[:].bitcast(I32)[k0 + r : P : 32, :], in_=rows[r : 16 : 4, :])
+            for r in range(PACK):
+                nc.sync.dma_start(out=plane[:].bitcast(I32)[first + r : P : QUADRANT, :], in_=rows[r:BLOCKS:PACK, :])
 
-        def load_rows(name, src, c0, c1, q):
-            t = sb(name, [P, PACK, c1 - c0], F32)
-            q.dma_start(out=t[:], in_=src.rearrange("(p t) c -> p t c", t=PACK)[:, :, c0:c1])
-            return t
+        def load_rows(name, src, cols):
+            rows = src.rearrange("(p t) c -> p t c", t=PACK)[:, :, cols]
+            return load(name, rows, [P, PACK, cols.stop - cols.start], F32, nc.sync)
 
-        def load_plain(name, src, shape, dtype, q):
-            t = sb(name, shape, dtype)
-            q.dma_start(out=t[:], in_=src)
-            return t
+        def interleave(copy, woven, raw, cols):
+            copy(
+                out=woven[:, cols, :].rearrange("p (c i) t -> p c t i", i=LINE),
+                in_=raw[:, :, cols].rearrange("p t (c i) -> p c t i", i=LINE),
+            )
 
-        def weave(dst, raw, c0, c1, eng):
-            o = dst[:, c0:c1, :].rearrange("p (c i) t -> p c t i", i=4)
-            s = raw[:, :, c0:c1].rearrange("p t (c i) -> p c t i", i=4)
-            if eng == "v":
-                nc.vector.tensor_copy(out=o, in_=s)
-            elif eng == "g":
-                nc.gpsimd.tensor_scalar(out=o, in0=s, scalar1=1.0, scalar2=0.0, op0=ALU.mult, op1=ALU.add)
-            else:
-                nc.scalar.copy(out=o, in_=s)
+        def quantise(name, woven, width):
+            words = sbuf(name + "_words", [P, width], U32)
+            plane = sbuf(name + "_plane", [P, width], U8)
+            nc.vector.quantize_mx(out=words[:].bitcast(FP8X4), scales=plane[:], in_=woven[:].rearrange("p c t -> p (c t)"))
+            return words, plane
 
-        def quant(name, woven, n):
-            codes = sb(name + "_codes", [P, n], U32)
-            sc = sb(name + "_sc", [P, n], U8)
-            nc.vector.quantize_mx(out=codes[:].bitcast(FP8X4), scales=sc[:], in_=woven[:].rearrange("p c t -> p (c t)"))
-            return codes, sc
+        def gather(name, window, offsets, slots, dtype):
+            picked = sbuf(name, [P, slots.stop - slots.start], dtype)
+            entries = offsets[:, slots.start // PER_COLUMN : slots.stop // PER_COLUMN]
+            nc.vector.tensor_copy(out=picked[:], in_=window.indirect(entries))
+            return picked
 
-        def gather(name, window, lst, c0, c1, dtype):
-            g = sb(name, [P, c1 - c0], dtype)
-            w = window[:].bitcast(U32) if dtype == U32 else window[:]
-            nc.vector.tensor_copy(out=g[:], in_=w.indirect(lst[:, c0 // 16 : c1 // 16]))
-            return g
+        def product(name, width, weight, words, plane):
+            bank = psum.tile([P, width], F32, name=name)
+            nc.tensor.matmul_mx(
+                out=bank[:],
+                lhsT=weight[0][:].bitcast(FP8X4),
+                lhsT_scale=weight[1][:],
+                rhs=words.bitcast(FP8X4),
+                rhs_scale=plane,
+                start=True,
+                stop=True,
+            )
+            return bank
 
-        def mm(name, n, lhs, lhs_sc, rhs, rhs_sc):
-            acc = psum.tile([P, n], F32, name=name)
-            nc.tensor.matmul_mx(out=acc[:], lhsT=lhs.bitcast(FP8X4), lhsT_scale=lhs_sc, rhs=rhs.bitcast(FP8X4), rhs_scale=rhs_sc, start=True, stop=True)
-            return acc
+        all_r = slice(0, R)
+        all_j = slice(0, J)
 
+        tab2_plane = zeroed_plane("tab2_plane", nc.gpsimd)
+        tab_plane = zeroed_plane("tab_plane", nc.vector)
 
-        s2 = zero_plane("s2", nc.gpsimd)
-        s1 = zero_plane("s1", nc.vector)
-        warm = sb("warm", [P, 1], F32)
-        warm2 = sb("warm2", [P, 1], F32)
-        nc.vector.memset(warm[:], 0.0)
-        nc.scalar.activation(out=warm2[:], in_=warm[:], func=ACT.Tanh)
+        list2 = load("list2", offs2, [P, J // PER_COLUMN], U16, nc.sync)
+        w2_raw = load_rows("w2_raw", w2, all_r)
+        w1_raw = load_rows("w1_raw", w1, all_r)
+        load_scale_rows(tab2_plane, tab2_scales, 0)
+        tab2_window = load_words("tab2_window", tab2_words)
+        list1 = load("list1", offs, [P, J // PER_COLUMN], U16, nc.sync)
+        load_scale_rows(tab_plane, tab_scales, TAB_FIRST)
+        tab_window = load_words("tab_window", tab_words)
+        wo_raw = load_rows("wo_raw", wo, all_r)
+        dy_raw = [load_rows("dy_raw%d" % i, dy, chunk) for i, chunk in enumerate(CHUNKS)]
+        base_sb = load("base_sb", base, [P, J], F32, nc.sync)
+        bias_sb = load("bias_sb", bias, [P, 1], F32, nc.gpsimd)
+        og_sb = load("og_sb", og, [P, 1], F32, nc.gpsimd)
 
-        l2 = load_plain("l2", offs2, [P, J // 16], U16, nc.sync)
-        wor = load_rows("wor", wo, 0, R, nc.sync)
-        w2r = load_rows("w2r", w2, 0, R, nc.sync)
-        load_scales(s2, tab2_scales, nc.sync, 0)
-        dyr = load_rows("dyr", dy, 0, J, nc.sync)
-        l1 = load_plain("l1", offs, [P, J // 16], U16, nc.sync)
-        tw2 = load_words("tw2", tab2_words, nc.sync)
-        load_scales(s1, tab_scales, nc.sync, 4)
-        w1r = load_rows("w1r", w1, 0, R, nc.sync)
-        tw1 = load_words("tw1", tab_words, nc.sync)
-        base_t = load_plain("base_t", base, [P, J], F32, nc.sync)
-        bias_t = load_plain("bias_t", bias, [P, 1], F32, nc.gpsimd)
-        og_t = load_plain("og_t", og, [P, 1], F32, nc.gpsimd)
+        half_bias = sbuf("half_bias", [P, 1], F32)
+        nc.gpsimd.tensor_scalar(out=half_bias[:], in0=bias_sb[:], scalar1=-0.5, scalar2=0.0, op0=ALU.mult, op1=ALU.add)
 
-        nb = sb("nb", [P, 1], F32)
-        nc.gpsimd.tensor_scalar(out=nb[:], in0=bias_t[:], scalar1=-0.5, scalar2=0.0, op0=ALU.mult, op1=ALU.add)
-        halves = [slice(0, 256), slice(256, 512)]
-        wow = sb("wow", [P, R, PACK], BF16)
-        weave(wow, wor, 0, R, "s")
-        w2w = sb("w2w", [P, R, PACK], BF16)
-        weave(w2w, w2r, 0, R, "s")
-        gs2 = gather("gs2", s2, l2, 0, J, U8)
-        woc, wos = quant("woq", wow, R)
-        w2c, w2s = quant("w2q", w2w, R)
-        dw = sb("dw", [P, J, PACK], BF16)
-        weave(dw, dyr, 0, 192, "s")
-        weave(dw, dyr, 192, J, "v")
-        dc, ds = quant("dq", dw, J)
-        cacc = mm("cacc", J, woc[:], wos[:], dc[:], ds[:])
-        c2 = sb("c2", [P, J], F32)
-        nc.scalar.activation(out=c2[:], in_=cacc[:], func=ACT.Square)
-        tn = sb("tn", [P, J], F32)
-        baccs = []
-        for i, hs in enumerate(halves):
-            g = gather("gw2_%d" % i, tw2, l2, hs.start, hs.stop, U32)
-            baccs.append(mm("bacc%d" % i, 256, w2c[:], w2s[:], g[:], gs2[:, hs]))
-        w1w = sb("w1w", [P, R, PACK], BF16)
-        weave(w1w, w1r, 0, R, "s")
-        gs1 = gather("gs1", s1, l1, 0, J, U8)
-        w1c, w1s = quant("w1q", w1w, R)
-        q = sb("q", [P, J], F32)
-        u = sb("u", [P, J], F32)
-        root = math.sqrt(0.125)
-        for i, hs in enumerate(halves):
-            nc.scalar.activation(out=tn[:, hs], in_=baccs[i][:], func=ACT.Tanh, bias=nb[:], scale=-0.5)
-        for hs in halves:
-            nc.scalar.activation(out=q[:, hs], in_=tn[:, hs], func=ACT.Square)
-        for hs in halves:
-            nc.scalar.activation(out=u[:, hs], in_=q[:, hs], func=ACT.Square, bias=root, scale=-root)
-        gw1 = [gather("gw1_%d" % i, tw1, l1, hs.start, hs.stop, U32) for i, hs in enumerate(halves)]
-        pt = sb("pt", [P, J], F32)
-        qq = sb("qq", [P, J], F32)
-        for hs in halves:
-            nc.vector.tensor_tensor(out=pt[:, hs], in0=tn[:, hs], in1=c2[:, hs], op=ALU.mult)
-        for hs in halves:
-            nc.vector.tensor_tensor(out=qq[:, hs], in0=pt[:, hs], in1=u[:, hs], op=ALU.mult)
-        h = sb("h", [P, J], F32)
-        h2 = sb("h2", [P, J], F32)
-        r = sb("r", [P, J], F32)
-        res = sb("res", [P, J], F32)
-        cuts = [0,128,256,384,512]
-        pieces = [slice(c, e) for c, e in zip(cuts, cuts[1:])]
-        for half in range(2):
-            pair = pieces[2 * half : 2 * half + 2]
-            for i, cs in enumerate(pair):
-                acc = mm("aacc%d" % (2 * half + i), 128, w1c[:], w1s[:], gw1[half][:, 128 * i : 128 * (i + 1)], gs1[4:P, cs])
-                nc.scalar.activation(out=h[:, cs], in_=acc[:], func=ACT.Tanh)
-            for cs in pair:
-                nc.scalar.activation(out=h2[:, cs], in_=h[:, cs], func=ACT.Square)
-            for cs in pair:
-                nc.vector.tensor_tensor(out=r[:, cs], in0=h2[:, cs], in1=qq[:, cs], op=ALU.mult)
-            for cs in pair:
-                nc.vector.scalar_tensor_tensor(out=res[:, cs], in0=r[:, cs], scalar=og_t[:], in1=base_t[:, cs], op0=ALU.mult, op1=ALU.add)
-            nc.sync.dma_start(out=out[:, halves[half]], in_=res[:, halves[half]])
+        w2_woven = sbuf("w2_woven", [P, R, PACK], BF16)
+        interleave(nc.scalar.copy, w2_woven, w2_raw, all_r)
+        tab2_picked_plane = gather("tab2_picked_plane", tab2_plane[:], list2, all_j, U8)
+        tab2_picked = gather("tab2_picked", tab2_window[:].bitcast(U32), list2, all_j, U32)
+        w2_mx = quantise("w2", w2_woven, R)
+        b_bank = product("b_bank", J, w2_mx, tab2_picked[:], tab2_picked_plane[:])
+        w1_woven = sbuf("w1_woven", [P, R, PACK], BF16)
+        interleave(nc.scalar.copy, w1_woven, w1_raw, all_r)
+        tab_picked_plane = gather("tab_picked_plane", tab_plane[:], list1, all_j, U8)
+        w1_mx = quantise("w1", w1_woven, R)
+        tn = sbuf("tn", [P, J], F32)
+        nc.scalar.activation(out=tn[:], in_=b_bank[:], func=ACT.Tanh, bias=half_bias[:], scale=-0.5)
+        tn_sq = sbuf("tn_sq", [P, J], F32)
+        nc.scalar.activation(out=tn_sq[:], in_=tn[:], func=ACT.Square)
+
+        tab_picked = [gather("tab_picked%d" % i, tab_window[:].bitcast(U32), list1, half, U32) for i, half in enumerate(HALVES)]
+        wo_woven = sbuf("wo_woven", [P, R, PACK], BF16)
+        interleave(nc.scalar.copy, wo_woven, wo_raw, all_r)
+        wo_mx = quantise("wo", wo_woven, R)
+        h1 = sbuf("h1", [P, J], F32)
+        slope_sq = sbuf("slope_sq", [P, J], F32)
+        factor = sbuf("factor", [P, J], F32)
+        slope = sbuf("slope", [P, J], F32)
+        for i, half in enumerate(HALVES):
+            a_bank = product("a_bank%d" % i, J // 2, w1_mx, tab_picked[i][:], tab_picked_plane[TAB_FIRST:P, half])
+            nc.scalar.activation(out=h1[:, half], in_=a_bank[:], func=ACT.Tanh)
+            nc.vector.scalar_tensor_tensor(out=slope[:, half], in0=tn_sq[:, half], scalar=-1.0, in1=h1[:, half], op0=ALU.add, op1=ALU.mult)
+        for half in HALVES:
+            nc.scalar.activation(out=slope_sq[:, half], in_=slope[:, half], func=ACT.Square, scale=math.sqrt(0.125))
+            nc.vector.scalar_tensor_tensor(out=factor[:, half], in0=tn[:, half], scalar=og_sb[:], in1=slope_sq[:, half], op0=ALU.mult, op1=ALU.mult)
+
+        c0_sq = sbuf("c0_sq", [P, J], F32)
+        penalty = sbuf("penalty", [P, J], F32)
+        result = sbuf("result", [P, J], F32)
+        c0_banks = []
+        for i, chunk in enumerate(CHUNKS):
+            width = chunk.stop - chunk.start
+            dy_woven = sbuf("dy_woven%d" % i, [P, width, PACK], BF16)
+            interleave(nc.scalar.copy, dy_woven, dy_raw[i], slice(0, ON_SCALAR[i]))
+            if ON_SCALAR[i] < width:
+                interleave(nc.vector.tensor_copy, dy_woven, dy_raw[i], slice(ON_SCALAR[i], width))
+            dy_words, dy_plane = quantise("dy%d" % i, dy_woven, width)
+            c0_banks.append(product("c0_bank%d" % i, width, wo_mx, dy_words[:], dy_plane[:]))
+        for c0_bank, chunk in zip(c0_banks, CHUNKS):
+            nc.scalar.activation(out=c0_sq[:, chunk], in_=c0_bank[:], func=ACT.Square)
+            nc.vector.tensor_tensor(out=penalty[:, chunk], in0=c0_sq[:, chunk], in1=factor[:, chunk], op=ALU.mult)
+            nc.vector.tensor_tensor(out=result[:, chunk], in0=penalty[:, chunk], in1=base_sb[:, chunk], op=ALU.add)
+            nc.sync.dma_start(out=out[:, chunk], in_=result[:, chunk])

import math
from contextlib import ExitStack

import concourse.mybir as mybir

K, R, T, J = 512, 128, 2048, 512
FLOPS = 3 * 2 * K * R * J

F32 = mybir.dt.float32
BF16 = mybir.dt.bfloat16
I32 = mybir.dt.int32
U32 = mybir.dt.uint32
U16 = mybir.dt.uint16
U8 = mybir.dt.uint8
FP8X4 = mybir.dt.float8_e4m3fn_x4
ACT = mybir.ActivationFunctionType
ALU = mybir.AluOpType

P = 128
QUADRANT = 32
BLOCKS = K // 32
PACK = 4
LINE = 4
PER_COLUMN = 16
TAB_FIRST = 4

HALVES = [slice(0, J // 2), slice(J // 2, J)]
CHUNKS = [slice(0, 256), slice(256, 384), slice(384, 512)]
ON_SCALAR = [128, 128, 64]


def tile_attend_gptwotables_kernel(tc, tab_words, tab_scales, w1, tab2_words, tab2_scales, w2, bias, wo, dy, og, base, offs, offs2, out):
    nc = tc.nc
    with ExitStack() as ctx:
        keep = ctx.enter_context(tc.tile_pool(name="keep", bufs=1))
        psum = ctx.enter_context(tc.psum_pool(name="psum", bufs=1))

        def sbuf(name, shape, dtype):
            return keep.tile(shape, dtype, name=name, align_bytes=64)

        def load(name, src, shape, dtype, queue):
            tile = sbuf(name, shape, dtype)
            queue.dma_start(out=tile[:], in_=src)
            return tile

        def load_words(name, words):
            return load(name, words[0].rearrange("p n t -> p (n t)").bitcast(I32), [P, T], I32, nc.sync)

        def zeroed_plane(name, engine):
            plane = sbuf(name, [P, T], U8)
            engine.memset(plane[:].bitcast(I32), 0)
            return plane

        def load_scale_rows(plane, scales, first):
            rows = scales[0].bitcast(I32)
            for r in range(PACK):
                nc.sync.dma_start(out=plane[:].bitcast(I32)[first + r : P : QUADRANT, :], in_=rows[r:BLOCKS:PACK, :])

        def load_rows(name, src, cols):
            rows = src.rearrange("(p t) c -> p t c", t=PACK)[:, :, cols]
            return load(name, rows, [P, PACK, cols.stop - cols.start], F32, nc.sync)

        def interleave(copy, woven, raw, cols):
            copy(
                out=woven[:, cols, :].rearrange("p (c i) t -> p c t i", i=LINE),
                in_=raw[:, :, cols].rearrange("p t (c i) -> p c t i", i=LINE),
            )

        def quantise(name, woven, width):
            words = sbuf(name + "_words", [P, width], U32)
            plane = sbuf(name + "_plane", [P, width], U8)
            nc.vector.quantize_mx(out=words[:].bitcast(FP8X4), scales=plane[:], in_=woven[:].rearrange("p c t -> p (c t)"))
            return words, plane

        def gather(name, window, offsets, slots, dtype):
            picked = sbuf(name, [P, slots.stop - slots.start], dtype)
            entries = offsets[:, slots.start // PER_COLUMN : slots.stop // PER_COLUMN]
            nc.vector.tensor_copy(out=picked[:], in_=window.indirect(entries))
            return picked

        def product(name, width, weight, words, plane):
            bank = psum.tile([P, width], F32, name=name)
            nc.tensor.matmul_mx(
                out=bank[:],
                lhsT=weight[0][:].bitcast(FP8X4),
                lhsT_scale=weight[1][:],
                rhs=words.bitcast(FP8X4),
                rhs_scale=plane,
                start=True,
                stop=True,
            )
            return bank

        all_r = slice(0, R)
        all_j = slice(0, J)

        tab2_plane = zeroed_plane("tab2_plane", nc.gpsimd)
        tab_plane = zeroed_plane("tab_plane", nc.vector)

        list2 = load("list2", offs2, [P, J // PER_COLUMN], U16, nc.sync)
        w2_raw = load_rows("w2_raw", w2, all_r)
        w1_raw = load_rows("w1_raw", w1, all_r)
        load_scale_rows(tab2_plane, tab2_scales, 0)
        tab2_window = load_words("tab2_window", tab2_words)
        list1 = load("list1", offs, [P, J // PER_COLUMN], U16, nc.sync)
        load_scale_rows(tab_plane, tab_scales, TAB_FIRST)
        tab_window = load_words("tab_window", tab_words)
        wo_raw = load_rows("wo_raw", wo, all_r)
        dy_raw = [load_rows("dy_raw%d" % i, dy, chunk) for i, chunk in enumerate(CHUNKS)]
        base_sb = load("base_sb", base, [P, J], F32, nc.sync)
        bias_sb = load("bias_sb", bias, [P, 1], F32, nc.gpsimd)
        og_sb = load("og_sb", og, [P, 1], F32, nc.gpsimd)

        half_bias = sbuf("half_bias", [P, 1], F32)
        nc.gpsimd.tensor_scalar(out=half_bias[:], in0=bias_sb[:], scalar1=-0.5, scalar2=0.0, op0=ALU.mult, op1=ALU.add)

        w2_woven = sbuf("w2_woven", [P, R, PACK], BF16)
        interleave(nc.scalar.copy, w2_woven, w2_raw, all_r)
        tab2_picked_plane = gather("tab2_picked_plane", tab2_plane[:], list2, all_j, U8)
        tab2_picked = gather("tab2_picked", tab2_window[:].bitcast(U32), list2, all_j, U32)
        w2_mx = quantise("w2", w2_woven, R)
        b_bank = product("b_bank", J, w2_mx, tab2_picked[:], tab2_picked_plane[:])
        w1_woven = sbuf("w1_woven", [P, R, PACK], BF16)
        interleave(nc.scalar.copy, w1_woven, w1_raw, all_r)
        tab_picked_plane = gather("tab_picked_plane", tab_plane[:], list1, all_j, U8)
        w1_mx = quantise("w1", w1_woven, R)
        tn = sbuf("tn", [P, J], F32)
        nc.scalar.activation(out=tn[:], in_=b_bank[:], func=ACT.Tanh, bias=half_bias[:], scale=-0.5)
        tn_sq = sbuf("tn_sq", [P, J], F32)
        nc.scalar.activation(out=tn_sq[:], in_=tn[:], func=ACT.Square)

        tab_picked = [gather("tab_picked%d" % i, tab_window[:].bitcast(U32), list1, half, U32) for i, half in enumerate(HALVES)]
        wo_woven = sbuf("wo_woven", [P, R, PACK], BF16)
        interleave(nc.scalar.copy, wo_woven, wo_raw, all_r)
        wo_mx = quantise("wo", wo_woven, R)
        h1 = sbuf("h1", [P, J], F32)
        slope_sq = sbuf("slope_sq", [P, J], F32)
        factor = sbuf("factor", [P, J], F32)
        slope = sbuf("slope", [P, J], F32)
        for i, half in enumerate(HALVES):
            a_bank = product("a_bank%d" % i, J // 2, w1_mx, tab_picked[i][:], tab_picked_plane[TAB_FIRST:P, half])
            nc.scalar.activation(out=h1[:, half], in_=a_bank[:], func=ACT.Tanh)
            nc.vector.scalar_tensor_tensor(out=slope[:, half], in0=tn_sq[:, half], scalar=-1.0, in1=h1[:, half], op0=ALU.add, op1=ALU.mult)
        for half in HALVES:
            nc.scalar.activation(out=slope_sq[:, half], in_=slope[:, half], func=ACT.Square, scale=math.sqrt(0.125))
            nc.vector.scalar_tensor_tensor(out=factor[:, half], in0=tn[:, half], scalar=og_sb[:], in1=slope_sq[:, half], op0=ALU.mult, op1=ALU.mult)

        c0_sq = sbuf("c0_sq", [P, J], F32)
        penalty = sbuf("penalty", [P, J], F32)
        result = sbuf("result", [P, J], F32)
        c0_banks = []
        for i, chunk in enumerate(CHUNKS):
            width = chunk.stop - chunk.start
            dy_woven = sbuf("dy_woven%d" % i, [P, width, PACK], BF16)
            interleave(nc.scalar.copy, dy_woven, dy_raw[i], slice(0, ON_SCALAR[i]))
            if ON_SCALAR[i] < width:
                interleave(nc.vector.tensor_copy, dy_woven, dy_raw[i], slice(ON_SCALAR[i], width))
            dy_words, dy_plane = quantise("dy%d" % i, dy_woven, width)
            c0_banks.append(product("c0_bank%d" % i, width, wo_mx, dy_words[:], dy_plane[:]))
        for c0_bank, chunk in zip(c0_banks, CHUNKS):
            nc.scalar.activation(out=c0_sq[:, chunk], in_=c0_bank[:], func=ACT.Square)
            nc.vector.tensor_tensor(out=penalty[:, chunk], in0=c0_sq[:, chunk], in1=factor[:, chunk], op=ALU.mult)
            nc.vector.tensor_tensor(out=result[:, chunk], in0=penalty[:, chunk], in1=base_sb[:, chunk], op=ALU.add)
            nc.sync.dma_start(out=out[:, chunk], in_=result[:, chunk])
